import numpy as np
import ml_dtypes


def mxq(x, axis, fmt="e4m3"):
    dtype, down = {"e4m3": (ml_dtypes.float8_e4m3fn, 7), "e5m2": (ml_dtypes.float8_e5m2, 14)}[fmt]
    v = np.moveaxis(np.asarray(x, np.float32).astype(ml_dtypes.bfloat16).astype(np.float64), axis, -1)
    blocks = v.reshape(v.shape[:-1] + (-1, 32))
    amax = np.abs(blocks).max(-1, keepdims=True)
    byte = np.maximum(np.where(amax > 0, np.frexp(amax)[1] - 1 + 127, 0) - down, 1)
    scale = np.exp2(byte - 127.0)
    codes = (blocks / scale).astype(np.float32).astype(dtype).astype(np.float64)
    return np.moveaxis((codes * scale).reshape(v.shape), -1, axis)


WIDE = False


def mx_kscale(k):
    if not WIDE:
        return np.ones(k)
    levels = np.array([10, -10, 5, -5, 0])
    if k % 512:
        return np.exp2(np.random.permutation(np.resize(levels, k // 32))).repeat(32)
    a = np.empty((k // 512, 16))
    for p in range(k // 512):
        a[p, :8] = np.random.permutation(np.resize(levels, 8))
        for g in range(8):
            far = levels[np.abs(levels - a[p, g]) >= 10]
            a[p, g + 8] = far[np.random.randint(len(far))]
    return np.exp2(a.ravel()).repeat(32)


def f64(x):
    return np.asarray(x).astype(np.float64)


def striped(idx):
    return np.tile(np.asarray(idx).reshape(-1, 16).T, (8, 1)).astype(np.uint16)


def unstriped(offs):
    return offs[:16].T.reshape(-1).astype(np.int64)


E2M1 = np.array([0.0, 0.5, 1.0, 1.5, 2.0, 3.0, 4.0, 6.0, -0.0, -0.5, -1.0, -1.5, -2.0, -3.0, -4.0, -6.0])


def pack_weight(w, fmt):
    k, n = w.shape
    w = f64(np.asarray(w, np.float32).astype(ml_dtypes.bfloat16)).reshape(k // 32, 32, n)
    amax = np.abs(w).max(1)
    if fmt == "e4m3":
        byte = np.frexp(amax)[1] - 1 + 127 - 7
    else:
        mant, ex = np.frexp(amax / 6.0)
        byte = np.where(mant > 0.5, ex, ex - 1) + 127
    byte = np.clip(np.where(amax > 0, byte, 1), 1, 254)
    scaled = (w * np.exp2(127.0 - byte)[:, None, :]).reshape(k, n).astype(np.float32)
    by_word = np.ascontiguousarray(scaled.reshape(k // 512, 128, 4, n).transpose(0, 1, 3, 2))
    if fmt == "e4m3":
        words = by_word.astype(ml_dtypes.float8_e4m3fn).view(np.uint8)
    else:
        c = by_word.astype(ml_dtypes.float4_e2m1fn).view(np.uint8) & 0xF
        words = (c[..., 0::2] | (c[..., 1::2] << 4)).reshape(k // 512, 128, 2 * n)
    return np.ascontiguousarray(words), np.ascontiguousarray(byte.astype(np.uint8).reshape(k // 512, 16, n))


def unpack_weight(words, scales, fmt):
    g, _, n = scales.shape
    words = np.ascontiguousarray(words).reshape(g, 128, n, -1)
    if fmt == "e4m3":
        vals = words.view(ml_dtypes.float8_e4m3fn).astype(np.float64)
    else:
        nib = np.empty((g, 128, n, 4), np.uint8)
        nib[..., 0::2] = words & 0xF
        nib[..., 1::2] = words >> 4
        vals = E2M1[nib]
    vals = vals * np.repeat(np.exp2(scales.astype(np.float64) - 127.0), 8, axis=1)[..., None]
    return vals.transpose(0, 1, 3, 2).reshape(g * 512, n)


D, T, I, Q = 512, 2048, 512, 128


def setup_inputs():
    n = np.random.standard_normal
    idx = np.random.permutation(T)[:I]
    fd = mx_kscale(D)
    keysp = pack_weight(n((D, T)) / fd[:, None], "e2m1")
    return {
        "query": (n((D, Q)) * 0.5 / np.sqrt(D) * fd[:, None]).astype(np.float32),
        "keys_words": keysp[0],
        "keys_scales": keysp[1],
        "counts": (np.random.uniform(0.0, 2.0, (Q, T))).astype(np.float32),
        "weary": (np.random.uniform(0.2, 0.8, (Q, 1))).astype(np.float32),
        "offs": striped(idx),
    }


def reference(query, keys_words, keys_scales, counts, weary, offs):
    idx = unstriped(offs)
    keysu = unpack_weight(keys_words, keys_scales, "e2m1")
    queryq = mxq(f64(query), 0, "e4m3")
    keysidxg = keysu[:, idx]
    a = queryq.T @ keysidxg
    s = a - f64(counts)[:, idx] * f64(weary)
    p = np.exp(s - np.max(s, axis=1, keepdims=True))
    w = p / np.sum(p, axis=1, keepdims=True) * 512.0
    wf = np.zeros((Q, T))
    wf[:, idx] = w
    y = f64(counts) + wf
    return y

@@ -1,0 +1,122 @@
+from contextlib import ExitStack
+
+import concourse.mybir as mybir
+
+D, T, I, Q = 512, 2048, 512, 128
+FLOPS = 2 * D * I * Q
+
+F32 = mybir.dt.float32
+BF16 = mybir.dt.bfloat16
+I32 = mybir.dt.int32
+U32 = mybir.dt.uint32
+U16 = mybir.dt.uint16
+U8 = mybir.dt.uint8
+FP8X4 = mybir.dt.float8_e4m3fn_x4
+FP4X4 = mybir.dt.float4_e2m1fn_x4
+ALU = mybir.AluOpType
+ACT = mybir.ActivationFunctionType
+AXIS = mybir.AxisListType
+
+P = 128
+PACK = 4
+STRIPE = 16
+HALVES = 2
+STORE_WIDTHS = (512, 512, 512, 384, 128)
+
+
+def tile_attend_readcounts_kernel(tc, query, keys_words, keys_scales, counts, weary, offs, out):
+    nc = tc.nc
+    with ExitStack() as ctx:
+        sb = ctx.enter_context(tc.tile_pool(name="sb", bufs=1))
+        ps = ctx.enter_context(tc.psum_pool(name="ps", bufs=1))
+
+        offsets = sb.tile([P, I // STRIPE], U16, name="offsets")
+        nc.sync.dma_start(offsets[:], offs)
+
+        seed = sb.tile([P, 1], F32, name="seed")
+        nc.gpsimd.memset(seed[:], 0.0)
+        warm = sb.tile([P, 1], F32, name="warm")
+        nc.scalar.activation(warm[:], seed[:], ACT.Exp)
+
+        pool_scales = sb.tile([P, T], U8, name="pool_scales", tag="scales_then_listed", align_bytes=64)
+        nc.vector.memset(pool_scales[:].bitcast(I32), 0)
+        placed = sb.tile([P, T], F32, name="placed", align_bytes=64)
+        nc.vector.memset(placed[:], 0.0)
+
+        for quad in range(4):
+            nc.scalar.dma_start(
+                pool_scales[32 * quad : 32 * quad + 4, :].bitcast(I32),
+                keys_scales[0, 4 * quad : 4 * quad + 4, :].bitcast(I32),
+            )
+        pool_words = sb.tile([P, T], U16, name="pool_words", align_bytes=64)
+        nc.sync.dma_start(pool_words[:].bitcast(I32), keys_words[0].bitcast(I32))
+        query_rows = sb.tile([P, PACK, Q], F32, name="query_rows", align_bytes=64)
+        nc.sync.dma_start(query_rows[:], query.rearrange("(p j) q -> p j q", j=PACK))
+        counts_sb = sb.tile([P, T], F32, name="counts_sb", align_bytes=64)
+        nc.sync.dma_start(counts_sb[:], counts)
+        weary_sb = sb.tile([P, 1], F32, name="weary_sb")
+        nc.sync.dma_start(weary_sb[:], weary)
+
+        key_scales = sb.tile([P, I], U8, name="key_scales", align_bytes=64)
+        nc.vector.tensor_copy(key_scales[:], pool_scales[:].indirect(offsets[:]))
+
+        query_bf = sb.tile([P, Q, PACK], BF16, name="query_bf", align_bytes=64)
+        nc.scalar.copy(query_bf[:], query_rows[:].rearrange("p j q -> p q j"))
+        query_codes = sb.tile([P, Q], U32, name="query_codes", align_bytes=64)
+        query_scales = sb.tile([P, Q], U8, name="query_scales", align_bytes=64)
+        nc.vector.quantize_mx(
+            out=query_codes[:].bitcast(FP8X4),
+            scales=query_scales[:],
+            in_=query_bf[:].rearrange("p q j -> p (q j)"),
+        )
+
+        key_words = sb.tile([P, I], U16, name="key_words", align_bytes=64)
+        nc.vector.tensor_copy(key_words[:], pool_words[:].indirect(offsets[:]))
+
+        scores = ps.tile([Q, I], F32, name="scores")
+        nc.tensor.matmul_mx(
+            out=scores[:],
+            lhsT=query_codes[:].bitcast(FP8X4),
+            lhsT_scale=query_scales[:],
+            rhs=key_words[:].bitcast(FP4X4),
+            rhs_scale=key_scales[:],
+            start=True,
+            stop=True,
+        )
+
+        listed = sb.tile([P, I], F32, name="listed", tag="scales_then_listed", align_bytes=64)
+        negated = sb.tile([P, I], F32, name="negated", align_bytes=64)
+        width = I // HALVES
+        for h in range(HALVES):
+            nc.vector.tensor_copy(
+                listed[:, h * width : (h + 1) * width],
+                counts_sb[:].indirect(offsets[:, h * width // STRIPE : (h + 1) * width // STRIPE]),
+            )
+        for h in range(HALVES):
+            cols = slice(h * width, (h + 1) * width)
+            nc.vector.scalar_tensor_tensor(
+                negated[:, cols], listed[:, cols], weary_sb[:], scores[:, cols], ALU.mult, ALU.subtract
+            )
+        least = sb.tile([P, 1], F32, name="least")
+        nc.vector.tensor_reduce(least[:], negated[:], AXIS.X, ALU.min)
+
+        p = sb.tile([P, I], F32, name="p", align_bytes=64)
+        row_sum = sb.tile([P, 1], F32, name="row_sum")
+        nc.scalar.activation(p[:], negated[:], ACT.Exp, bias=least[:], scale=-1.0, accum_out=row_sum[:])
+        share = sb.tile([P, 1], F32, name="share")
+        nc.scalar.activation(share[:], row_sum[:], ACT.Identity, scale=1.0 / 512.0)
+
+        nc.vector.tensor_copy(placed[:].indirect(offsets[:]), p[:])
+        factor = sb.tile([P, 1], F32, name="factor")
+        nc.vector.reciprocal(factor[:], share[:])
+
+        start = 0
+        for k, w in enumerate(STORE_WIDTHS):
+            cols = slice(start, start + w)
+            result = sb.tile([P, w], F32, name="result%d" % k, align_bytes=64)
+            nc.vector.scalar_tensor_tensor(
+                result[:], placed[:, cols], factor[:], counts_sb[:, cols], ALU.mult, ALU.add
+            )
+            queue = nc.sync if k % 2 == 0 else nc.scalar
+            queue.dma_start(out[:, cols], result[:])
+            start = start + w

@@ -33,29 +33,24 @@ def tile_attend_readcounts_kernel(tc, query, keys_words, keys_scales, counts, we
         offsets = sb.tile([P, I // STRIPE], U16, name="offsets")
         nc.sync.dma_start(offsets[:], offs)
 
-        seed = sb.tile([P, 1], F32, name="seed")
-        nc.gpsimd.memset(seed[:], 0.0)
-        warm = sb.tile([P, 1], F32, name="warm")
-        nc.scalar.activation(warm[:], seed[:], ACT.Exp)
-
         pool_scales = sb.tile([P, T], U8, name="pool_scales", tag="scales_then_listed", align_bytes=64)
         nc.vector.memset(pool_scales[:].bitcast(I32), 0)
         placed = sb.tile([P, T], F32, name="placed", align_bytes=64)
         nc.vector.memset(placed[:], 0.0)
 
-        for quad in range(4):
-            nc.scalar.dma_start(
-                pool_scales[32 * quad : 32 * quad + 4, :].bitcast(I32),
-                keys_scales[0, 4 * quad : 4 * quad + 4, :].bitcast(I32),
-            )
         pool_words = sb.tile([P, T], U16, name="pool_words", align_bytes=64)
         nc.sync.dma_start(pool_words[:].bitcast(I32), keys_words[0].bitcast(I32))
         query_rows = sb.tile([P, PACK, Q], F32, name="query_rows", align_bytes=64)
         nc.sync.dma_start(query_rows[:], query.rearrange("(p j) q -> p j q", j=PACK))
-        counts_sb = sb.tile([P, T], F32, name="counts_sb", align_bytes=64)
-        nc.sync.dma_start(counts_sb[:], counts)
         weary_sb = sb.tile([P, 1], F32, name="weary_sb")
         nc.sync.dma_start(weary_sb[:], weary)
+        for quad in range(4):
+            nc.sync.dma_start(
+                pool_scales[32 * quad : 32 * quad + 4, :].bitcast(I32),
+                keys_scales[0, 4 * quad : 4 * quad + 4, :].bitcast(I32),
+            )
+        counts_sb = sb.tile([P, T], F32, name="counts_sb", align_bytes=64)
+        nc.sync.dma_start(counts_sb[:], counts)
 
         key_scales = sb.tile([P, I], U8, name="key_scales", align_bytes=64)
         nc.vector.tensor_copy(key_scales[:], pool_scales[:].indirect(offsets[:]))

@@ -21,7 +21,7 @@ P = 128
 PACK = 4
 STRIPE = 16
 HALVES = 2
-STORE_WIDTHS = (512, 512, 512, 384, 128)
+STORE_WIDTHS = (256, 384, 448, 448, 512)
 
 
 def tile_attend_readcounts_kernel(tc, query, keys_words, keys_scales, counts, weary, offs, out):
@@ -30,27 +30,28 @@ def tile_attend_readcounts_kernel(tc, query, keys_words, keys_scales, counts, we
         sb = ctx.enter_context(tc.tile_pool(name="sb", bufs=1))
         ps = ctx.enter_context(tc.psum_pool(name="ps", bufs=1))
 
+        pool_words = sb.tile([P, T], U16, name="pool_words", align_bytes=64)
+        nc.sync.dma_start(pool_words[:].bitcast(I32), keys_words[0].bitcast(I32))
         offsets = sb.tile([P, I // STRIPE], U16, name="offsets")
         nc.sync.dma_start(offsets[:], offs)
 
-        pool_scales = sb.tile([P, T], U8, name="pool_scales", tag="scales_then_listed", align_bytes=64)
-        nc.vector.memset(pool_scales[:].bitcast(I32), 0)
+        pool_scales = sb.tile([P, T], U8, name="pool_scales", align_bytes=64)
+        nc.vector.memset(pool_scales[:, : T // 2].bitcast(I32), 0)
+        nc.gpsimd.memset(pool_scales[:, T // 2 :].bitcast(I32), 0)
         placed = sb.tile([P, T], F32, name="placed", align_bytes=64)
-        nc.vector.memset(placed[:], 0.0)
+        nc.vector.memset(placed[:].bitcast(I32), 0)
 
-        pool_words = sb.tile([P, T], U16, name="pool_words", align_bytes=64)
-        nc.sync.dma_start(pool_words[:].bitcast(I32), keys_words[0].bitcast(I32))
         query_rows = sb.tile([P, PACK, Q], F32, name="query_rows", align_bytes=64)
         nc.sync.dma_start(query_rows[:], query.rearrange("(p j) q -> p j q", j=PACK))
-        weary_sb = sb.tile([P, 1], F32, name="weary_sb")
-        nc.sync.dma_start(weary_sb[:], weary)
-        for quad in range(4):
+        for row in range(4):
             nc.sync.dma_start(
-                pool_scales[32 * quad : 32 * quad + 4, :].bitcast(I32),
-                keys_scales[0, 4 * quad : 4 * quad + 4, :].bitcast(I32),
+                pool_scales[row:P:32, :].bitcast(I32),
+                keys_scales[0, row:16:4, :].bitcast(I32),
             )
         counts_sb = sb.tile([P, T], F32, name="counts_sb", align_bytes=64)
         nc.sync.dma_start(counts_sb[:], counts)
+        weary_sb = sb.tile([P, 1], F32, name="weary_sb")
+        nc.sync.dma_start(weary_sb[:], weary)
 
         key_scales = sb.tile([P, I], U8, name="key_scales", align_bytes=64)
         nc.vector.tensor_copy(key_scales[:], pool_scales[:].indirect(offsets[:]))
@@ -79,7 +80,7 @@ def tile_attend_readcounts_kernel(tc, query, keys_words, keys_scales, counts, we
             stop=True,
         )
 
-        listed = sb.tile([P, I], F32, name="listed", tag="scales_then_listed", align_bytes=64)
+        listed = sb.tile([P, I], F32, name="listed", align_bytes=64)
         negated = sb.tile([P, I], F32, name="negated", align_bytes=64)
         width = I // HALVES
         for h in range(HALVES):

@@ -30,8 +30,6 @@ def tile_attend_readcounts_kernel(tc, query, keys_words, keys_scales, counts, we
         sb = ctx.enter_context(tc.tile_pool(name="sb", bufs=1))
         ps = ctx.enter_context(tc.psum_pool(name="ps", bufs=1))
 
-        pool_words = sb.tile([P, T], U16, name="pool_words", align_bytes=64)
-        nc.sync.dma_start(pool_words[:].bitcast(I32), keys_words[0].bitcast(I32))
         offsets = sb.tile([P, I // STRIPE], U16, name="offsets")
         nc.sync.dma_start(offsets[:], offs)
 
@@ -43,18 +41,24 @@ def tile_attend_readcounts_kernel(tc, query, keys_words, keys_scales, counts, we
 
         query_rows = sb.tile([P, PACK, Q], F32, name="query_rows", align_bytes=64)
         nc.sync.dma_start(query_rows[:], query.rearrange("(p j) q -> p j q", j=PACK))
-        for row in range(4):
-            nc.sync.dma_start(
-                pool_scales[row:P:32, :].bitcast(I32),
-                keys_scales[0, row:16:4, :].bitcast(I32),
-            )
-        counts_sb = sb.tile([P, T], F32, name="counts_sb", align_bytes=64)
-        nc.sync.dma_start(counts_sb[:], counts)
         weary_sb = sb.tile([P, 1], F32, name="weary_sb")
         nc.sync.dma_start(weary_sb[:], weary)
+        nc.sync.dma_start(pool_scales[0:P:8, :].bitcast(I32), keys_scales[0].bitcast(I32))
+        pool_words = sb.tile([P, T], U16, name="pool_words", align_bytes=64)
+        nc.sync.dma_start(pool_words[:].bitcast(I32), keys_words[0].bitcast(I32))
+        counts_sb = sb.tile([P, T], F32, name="counts_sb", align_bytes=64)
+        nc.sync.dma_start(counts_sb[:], counts)
 
+        listed_scales = sb.tile([P, I], U8, name="listed_scales", align_bytes=64)
+        nc.vector.tensor_copy(listed_scales[:], pool_scales[:].indirect(offsets[:]))
         key_scales = sb.tile([P, I], U8, name="key_scales", align_bytes=64)
-        nc.vector.tensor_copy(key_scales[:], pool_scales[:].indirect(offsets[:]))
+        nc.gpsimd.memset(key_scales[:].bitcast(I32), 0)
+        for row in range(4):
+            queue = nc.sync if row % 2 == 0 else nc.scalar
+            queue.dma_start(
+                key_scales[row:P:32, :].bitcast(I32),
+                listed_scales[8 * row : P : 32, :].bitcast(I32),
+            )
 
         query_bf = sb.tile([P, Q, PACK], BF16, name="query_bf", align_bytes=64)
         nc.scalar.copy(query_bf[:], query_rows[:].rearrange("p j q -> p q j"))
@@ -69,20 +73,24 @@ def tile_attend_readcounts_kernel(tc, query, keys_words, keys_scales, counts, we
         key_words = sb.tile([P, I], U16, name="key_words", align_bytes=64)
         nc.vector.tensor_copy(key_words[:], pool_words[:].indirect(offsets[:]))
 
-        scores = ps.tile([Q, I], F32, name="scores")
-        nc.tensor.matmul_mx(
-            out=scores[:],
-            lhsT=query_codes[:].bitcast(FP8X4),
-            lhsT_scale=query_scales[:],
-            rhs=key_words[:].bitcast(FP4X4),
-            rhs_scale=key_scales[:],
-            start=True,
-            stop=True,
-        )
+        width = I // HALVES
+        scores = []
+        for h in range(HALVES):
+            cols = slice(h * width, (h + 1) * width)
+            bank = ps.tile([Q, width], F32, name="scores%d" % h)
+            nc.tensor.matmul_mx(
+                out=bank[:],
+                lhsT=query_codes[:].bitcast(FP8X4),
+                lhsT_scale=query_scales[:],
+                rhs=key_words[:, cols].bitcast(FP4X4),
+                rhs_scale=key_scales[:, cols],
+                start=True,
+                stop=True,
+            )
+            scores.append(bank)
 
         listed = sb.tile([P, I], F32, name="listed", align_bytes=64)
         negated = sb.tile([P, I], F32, name="negated", align_bytes=64)
-        width = I // HALVES
         for h in range(HALVES):
             nc.vector.tensor_copy(
                 listed[:, h * width : (h + 1) * width],
@@ -91,7 +99,7 @@ def tile_attend_readcounts_kernel(tc, query, keys_words, keys_scales, counts, we
         for h in range(HALVES):
             cols = slice(h * width, (h + 1) * width)
             nc.vector.scalar_tensor_tensor(
-                negated[:, cols], listed[:, cols], weary_sb[:], scores[:, cols], ALU.mult, ALU.subtract
+                negated[:, cols], listed[:, cols], weary_sb[:], scores[h][:], ALU.mult, ALU.subtract
             )
         least = sb.tile([P, 1], F32, name="least")
         nc.vector.tensor_reduce(least[:], negated[:], AXIS.X, ALU.min)

@@ -20,8 +20,14 @@ AXIS = mybir.AxisListType
 P = 128
 PACK = 4
 STRIPE = 16
+BLOCKS = D // 32
+QUADRANT = 32
+QUADRANT_BLOCKS = 4
+SCALE_ROW0 = P - BLOCKS
+WEIGHT_TOTAL = 512.0
 HALVES = 2
 STORE_WIDTHS = (256, 384, 448, 448, 512)
+assert sum(STORE_WIDTHS) == T
 
 
 def tile_attend_readcounts_kernel(tc, query, keys_words, keys_scales, counts, weary, offs, out):
@@ -34,30 +40,30 @@ def tile_attend_readcounts_kernel(tc, query, keys_words, keys_scales, counts, we
         nc.sync.dma_start(offsets[:], offs)
 
         pool_scales = sb.tile([P, T], U8, name="pool_scales", align_bytes=64)
-        nc.vector.memset(pool_scales[:, : T // 2].bitcast(I32), 0)
-        nc.gpsimd.memset(pool_scales[:, T // 2 :].bitcast(I32), 0)
+        nc.scalar.dma_start(pool_scales[SCALE_ROW0:P, :].bitcast(I32), keys_scales[0].bitcast(I32))
+        nc.vector.memset(pool_scales[0:SCALE_ROW0, :].bitcast(I32), 0)
+
         placed = sb.tile([P, T], F32, name="placed", align_bytes=64)
-        nc.vector.memset(placed[:].bitcast(I32), 0)
+        nc.vector.memset(placed[:, : T // 2].bitcast(I32), 0)
+        nc.gpsimd.memset(placed[:, T // 2 :].bitcast(I32), 0)
 
         query_rows = sb.tile([P, PACK, Q], F32, name="query_rows", align_bytes=64)
         nc.sync.dma_start(query_rows[:], query.rearrange("(p j) q -> p j q", j=PACK))
-        weary_sb = sb.tile([P, 1], F32, name="weary_sb")
-        nc.sync.dma_start(weary_sb[:], weary)
-        nc.sync.dma_start(pool_scales[0:P:8, :].bitcast(I32), keys_scales[0].bitcast(I32))
         pool_words = sb.tile([P, T], U16, name="pool_words", align_bytes=64)
         nc.sync.dma_start(pool_words[:].bitcast(I32), keys_words[0].bitcast(I32))
         counts_sb = sb.tile([P, T], F32, name="counts_sb", align_bytes=64)
         nc.sync.dma_start(counts_sb[:], counts)
+        weary_sb = sb.tile([P, 1], F32, name="weary_sb")
+        nc.sync.dma_start(weary_sb[:], weary)
 
         listed_scales = sb.tile([P, I], U8, name="listed_scales", align_bytes=64)
         nc.vector.tensor_copy(listed_scales[:], pool_scales[:].indirect(offsets[:]))
         key_scales = sb.tile([P, I], U8, name="key_scales", align_bytes=64)
         nc.gpsimd.memset(key_scales[:].bitcast(I32), 0)
-        for row in range(4):
-            queue = nc.sync if row % 2 == 0 else nc.scalar
-            queue.dma_start(
-                key_scales[row:P:32, :].bitcast(I32),
-                listed_scales[8 * row : P : 32, :].bitcast(I32),
+        for row in range(QUADRANT_BLOCKS):
+            nc.sync.dma_start(
+                key_scales[row:P:QUADRANT, :].bitcast(I32),
+                listed_scales[SCALE_ROW0 + row : P : QUADRANT_BLOCKS, :].bitcast(I32),
             )
 
         query_bf = sb.tile([P, Q, PACK], BF16, name="query_bf", align_bytes=64)
@@ -108,7 +114,7 @@ def tile_attend_readcounts_kernel(tc, query, keys_words, keys_scales, counts, we
         row_sum = sb.tile([P, 1], F32, name="row_sum")
         nc.scalar.activation(p[:], negated[:], ACT.Exp, bias=least[:], scale=-1.0, accum_out=row_sum[:])
         share = sb.tile([P, 1], F32, name="share")
-        nc.scalar.activation(share[:], row_sum[:], ACT.Identity, scale=1.0 / 512.0)
+        nc.scalar.activation(share[:], row_sum[:], ACT.Identity, scale=1.0 / WEIGHT_TOTAL)
 
         nc.vector.tensor_copy(placed[:].indirect(offsets[:]), p[:])
         factor = sb.tile([P, 1], F32, name="factor")

from contextlib import ExitStack

import concourse.mybir as mybir

D, T, I, Q = 512, 2048, 512, 128
FLOPS = 2 * D * I * Q

F32 = mybir.dt.float32
BF16 = mybir.dt.bfloat16
I32 = mybir.dt.int32
U32 = mybir.dt.uint32
U16 = mybir.dt.uint16
U8 = mybir.dt.uint8
FP8X4 = mybir.dt.float8_e4m3fn_x4
FP4X4 = mybir.dt.float4_e2m1fn_x4
ALU = mybir.AluOpType
ACT = mybir.ActivationFunctionType
AXIS = mybir.AxisListType

P = 128
PACK = 4
STRIPE = 16
BLOCKS = D // 32
QUADRANT = 32
QUADRANT_BLOCKS = 4
SCALE_ROW0 = P - BLOCKS
WEIGHT_TOTAL = 512.0
HALVES = 2
STORE_WIDTHS = (256, 384, 448, 448, 512)
assert sum(STORE_WIDTHS) == T


def tile_attend_readcounts_kernel(tc, query, keys_words, keys_scales, counts, weary, offs, out):
    nc = tc.nc
    with ExitStack() as ctx:
        sb = ctx.enter_context(tc.tile_pool(name="sb", bufs=1))
        ps = ctx.enter_context(tc.psum_pool(name="ps", bufs=1))

        offsets = sb.tile([P, I // STRIPE], U16, name="offsets")
        nc.sync.dma_start(offsets[:], offs)

        pool_scales = sb.tile([P, T], U8, name="pool_scales", align_bytes=64)
        nc.scalar.dma_start(pool_scales[SCALE_ROW0:P, :].bitcast(I32), keys_scales[0].bitcast(I32))
        nc.vector.memset(pool_scales[0:SCALE_ROW0, :].bitcast(I32), 0)

        placed = sb.tile([P, T], F32, name="placed", align_bytes=64)
        nc.vector.memset(placed[:, : T // 2].bitcast(I32), 0)
        nc.gpsimd.memset(placed[:, T // 2 :].bitcast(I32), 0)

        query_rows = sb.tile([P, PACK, Q], F32, name="query_rows", align_bytes=64)
        nc.sync.dma_start(query_rows[:], query.rearrange("(p j) q -> p j q", j=PACK))
        pool_words = sb.tile([P, T], U16, name="pool_words", align_bytes=64)
        nc.sync.dma_start(pool_words[:].bitcast(I32), keys_words[0].bitcast(I32))
        counts_sb = sb.tile([P, T], F32, name="counts_sb", align_bytes=64)
        nc.sync.dma_start(counts_sb[:], counts)
        weary_sb = sb.tile([P, 1], F32, name="weary_sb")
        nc.sync.dma_start(weary_sb[:], weary)

        listed_scales = sb.tile([P, I], U8, name="listed_scales", align_bytes=64)
        nc.vector.tensor_copy(listed_scales[:], pool_scales[:].indirect(offsets[:]))
        key_scales = sb.tile([P, I], U8, name="key_scales", align_bytes=64)
        nc.gpsimd.memset(key_scales[:].bitcast(I32), 0)
        for row in range(QUADRANT_BLOCKS):
            nc.sync.dma_start(
                key_scales[row:P:QUADRANT, :].bitcast(I32),
                listed_scales[SCALE_ROW0 + row : P : QUADRANT_BLOCKS, :].bitcast(I32),
            )

        query_bf = sb.tile([P, Q, PACK], BF16, name="query_bf", align_bytes=64)
        nc.scalar.copy(query_bf[:], query_rows[:].rearrange("p j q -> p q j"))
        query_codes = sb.tile([P, Q], U32, name="query_codes", align_bytes=64)
        query_scales = sb.tile([P, Q], U8, name="query_scales", align_bytes=64)
        nc.vector.quantize_mx(
            out=query_codes[:].bitcast(FP8X4),
            scales=query_scales[:],
            in_=query_bf[:].rearrange("p q j -> p (q j)"),
        )

        key_words = sb.tile([P, I], U16, name="key_words", align_bytes=64)
        nc.vector.tensor_copy(key_words[:], pool_words[:].indirect(offsets[:]))

        width = I // HALVES
        scores = []
        for h in range(HALVES):
            cols = slice(h * width, (h + 1) * width)
            bank = ps.tile([Q, width], F32, name="scores%d" % h)
            nc.tensor.matmul_mx(
                out=bank[:],
                lhsT=query_codes[:].bitcast(FP8X4),
                lhsT_scale=query_scales[:],
                rhs=key_words[:, cols].bitcast(FP4X4),
                rhs_scale=key_scales[:, cols],
                start=True,
                stop=True,
            )
            scores.append(bank)

        listed = sb.tile([P, I], F32, name="listed", align_bytes=64)
        negated = sb.tile([P, I], F32, name="negated", align_bytes=64)
        for h in range(HALVES):
            nc.vector.tensor_copy(
                listed[:, h * width : (h + 1) * width],
                counts_sb[:].indirect(offsets[:, h * width // STRIPE : (h + 1) * width // STRIPE]),
            )
        for h in range(HALVES):
            cols = slice(h * width, (h + 1) * width)
            nc.vector.scalar_tensor_tensor(
                negated[:, cols], listed[:, cols], weary_sb[:], scores[h][:], ALU.mult, ALU.subtract
            )
        least = sb.tile([P, 1], F32, name="least")
        nc.vector.tensor_reduce(least[:], negated[:], AXIS.X, ALU.min)

        p = sb.tile([P, I], F32, name="p", align_bytes=64)
        row_sum = sb.tile([P, 1], F32, name="row_sum")
        nc.scalar.activation(p[:], negated[:], ACT.Exp, bias=least[:], scale=-1.0, accum_out=row_sum[:])
        share = sb.tile([P, 1], F32, name="share")
        nc.scalar.activation(share[:], row_sum[:], ACT.Identity, scale=1.0 / WEIGHT_TOTAL)

        nc.vector.tensor_copy(placed[:].indirect(offsets[:]), p[:])
        factor = sb.tile([P, 1], F32, name="factor")
        nc.vector.reciprocal(factor[:], share[:])

        start = 0
        for k, w in enumerate(STORE_WIDTHS):
            cols = slice(start, start + w)
            result = sb.tile([P, w], F32, name="result%d" % k, align_bytes=64)
            nc.vector.scalar_tensor_tensor(
                result[:], placed[:, cols], factor[:], counts_sb[:, cols], ALU.mult, ALU.add
            )
            queue = nc.sync if k % 2 == 0 else nc.scalar
            queue.dma_start(out[:, cols], result[:])
            start = start + w
